import numpy as np
import ml_dtypes


def mxq(x, axis, fmt="e4m3"):
    dtype, down = {"e4m3": (ml_dtypes.float8_e4m3fn, 7), "e5m2": (ml_dtypes.float8_e5m2, 14)}[fmt]
    v = np.moveaxis(np.asarray(x, np.float32).astype(ml_dtypes.bfloat16).astype(np.float64), axis, -1)
    blocks = v.reshape(v.shape[:-1] + (-1, 32))
    amax = np.abs(blocks).max(-1, keepdims=True)
    byte = np.maximum(np.where(amax > 0, np.frexp(amax)[1] - 1 + 127, 0) - down, 1)
    scale = np.exp2(byte - 127.0)
    codes = (blocks / scale).astype(np.float32).astype(dtype).astype(np.float64)
    return np.moveaxis((codes * scale).reshape(v.shape), -1, axis)


WIDE = False


def mx_kscale(k):
    if not WIDE:
        return np.ones(k)
    levels = np.array([10, -10, 5, -5, 0])
    if k % 512:
        return np.exp2(np.random.permutation(np.resize(levels, k // 32))).repeat(32)
    a = np.empty((k // 512, 16))
    for p in range(k // 512):
        a[p, :8] = np.random.permutation(np.resize(levels, 8))
        for g in range(8):
            far = levels[np.abs(levels - a[p, g]) >= 10]
            a[p, g + 8] = far[np.random.randint(len(far))]
    return np.exp2(a.ravel()).repeat(32)


def f64(x):
    return np.asarray(x).astype(np.float64)


E2M1 = np.array([0.0, 0.5, 1.0, 1.5, 2.0, 3.0, 4.0, 6.0, -0.0, -0.5, -1.0, -1.5, -2.0, -3.0, -4.0, -6.0])


def pack_weight(w, fmt):
    k, n = w.shape
    w = f64(np.asarray(w, np.float32).astype(ml_dtypes.bfloat16)).reshape(k // 32, 32, n)
    amax = np.abs(w).max(1)
    if fmt == "e4m3":
        byte = np.frexp(amax)[1] - 1 + 127 - 7
    else:
        mant, ex = np.frexp(amax / 6.0)
        byte = np.where(mant > 0.5, ex, ex - 1) + 127
    byte = np.clip(np.where(amax > 0, byte, 1), 1, 254)
    scaled = (w * np.exp2(127.0 - byte)[:, None, :]).reshape(k, n).astype(np.float32)
    by_word = np.ascontiguousarray(scaled.reshape(k // 512, 128, 4, n).transpose(0, 1, 3, 2))
    if fmt == "e4m3":
        words = by_word.astype(ml_dtypes.float8_e4m3fn).view(np.uint8)
    else:
        c = by_word.astype(ml_dtypes.float4_e2m1fn).view(np.uint8) & 0xF
        words = (c[..., 0::2] | (c[..., 1::2] << 4)).reshape(k // 512, 128, 2 * n)
    return np.ascontiguousarray(words), np.ascontiguousarray(byte.astype(np.uint8).reshape(k // 512, 16, n))


def unpack_weight(words, scales, fmt):
    g, _, n = scales.shape
    words = np.ascontiguousarray(words).reshape(g, 128, n, -1)
    if fmt == "e4m3":
        vals = words.view(ml_dtypes.float8_e4m3fn).astype(np.float64)
    else:
        nib = np.empty((g, 128, n, 4), np.uint8)
        nib[..., 0::2] = words & 0xF
        nib[..., 1::2] = words >> 4
        vals = E2M1[nib]
    vals = vals * np.repeat(np.exp2(scales.astype(np.float64) - 127.0), 8, axis=1)[..., None]
    return vals.transpose(0, 1, 3, 2).reshape(g * 512, n)


O, K, M, T = 1024, 2560, 2048, 1024


def setup_inputs():
    n = np.random.standard_normal
    s = mx_kscale(K)[:, None]
    x = n((K, T)); x[:O] *= 6.0
    w = n((K, M)) / np.sqrt(K) / s; w[:O] /= 2.0
    p_w8 = pack_weight(w[:O], "e4m3")
    p_w4 = pack_weight(w[O:], "e2m1")
    return {
        "x": (x * s).astype(np.float32),
        "w8_words": p_w8[0],
        "w8_scales": p_w8[1],
        "w4_words": p_w4[0],
        "w4_scales": p_w4[1],
    }


def reference(x, w8_words, w8_scales, w4_words, w4_scales):
    x_ = mxq(f64(x), 0, "e4m3")
    w8_ = unpack_weight(w8_words, w8_scales, "e4m3")
    w4_ = unpack_weight(w4_words, w4_scales, "e2m1")
    y = w8_.T @ x_[:O] + w4_.T @ x_[O:]
    return y

@@ -1,0 +1,217 @@
+from contextlib import ExitStack
+
+import concourse.mybir as mybir
+
+O, K, M, T = 1024, 2560, 2048, 1024
+FLOPS = 2 * K * M * T
+
+F32 = mybir.dt.float32
+BF16 = mybir.dt.bfloat16
+I32 = mybir.dt.int32
+U32 = mybir.dt.uint32
+U8 = mybir.dt.uint8
+E4M3 = mybir.dt.float8_e4m3fn_x4
+E2M1 = mybir.dt.float4_e2m1fn_x4
+
+P = 128
+PASS = 512
+NT = 512
+HALF = M // 2
+TILES = HALF // P
+
+
+def tile_mix_outl_fm_none_kernel(tc, x, w8_words, w8_scales, w4_words, w4_scales, out):
+    nc = tc.nc
+    with ExitStack() as ctx:
+        keep = ctx.enter_context(tc.tile_pool(name="keep", bufs=1))
+        stage = ctx.enter_context(tc.tile_pool(name="stage", bufs=3))
+        res = ctx.enter_context(tc.tile_pool(name="res", bufs=12))
+        psum = ctx.enter_context(tc.psum_pool(name="psum", bufs=8))
+        ctx.enter_context(tc.manual_schedule())
+
+        raw, codes, scales = {}, {}, {}
+        for g in range(5):
+            for h in range(2):
+                raw[g, h] = keep.tile([P, 4, NT], F32, name="raw_%d_%d" % (g, h), align_bytes=256)
+                codes[g, h] = keep.tile([P, NT], U32, name="codes_%d_%d" % (g, h), align_bytes=256)
+                scales[g, h] = keep.tile([P, NT], U8, name="scales_%d_%d" % (g, h), align_bytes=256)
+        w8 = {}
+        for g in range(2):
+            for h in range(2):
+                w8[g, h] = keep.tile([P, HALF], U32, name="w8_%d_%d" % (g, h), align_bytes=256)
+        w4a = [keep.tile([P, 2 * HALF], U8, name="w4a_%d" % g, align_bytes=256) for g in range(3)]
+        w4b = keep.tile([P, 3, 2 * HALF], U8, name="w4b", align_bytes=256)
+        w4sa = keep.tile([P, 3, HALF], U8, name="w4sa", align_bytes=256)
+        w4sb = keep.tile([P, 3, HALF], U8, name="w4sb", align_bytes=256)
+        w8s = keep.tile([P, M], U8, name="w8s", align_bytes=256)
+        warm = keep.tile([P, 8], F32, name="warm")
+        warm2 = keep.tile([P, 8], F32, name="warm2")
+
+        nc.vector.memset(w4sa[:].rearrange("p g n -> p (g n)").bitcast(U32), 0)
+        nc.gpsimd.memset(warm[:], 0.0)
+        nc.gpsimd.memset(w8s[:].bitcast(U32), 0)
+        nc.gpsimd.memset(w4sb[:].rearrange("p g n -> p (g n)").bitcast(U32), 0)
+
+        def load_x(g, h):
+            rows = x[PASS * g : PASS * (g + 1), :].rearrange("(p j) t -> p j t", j=4)
+            nc.sync.dma_start(out=raw[g, h][:], in_=rows[:, :, NT * h : NT * (h + 1)])
+
+        def load_w8(g, h):
+            src = w8_words[g].rearrange("p n i -> p (n i)")[:, 4 * HALF * h : 4 * HALF * (h + 1)]
+            nc.sync.dma_start(out=w8[g, h][:].bitcast(I32), in_=src.bitcast(I32))
+
+        def load_w4a(g):
+            nc.sync.dma_start(out=w4a[g][:].bitcast(I32), in_=w4_words[g][:, 0 : 2 * HALF].bitcast(I32))
+
+        def load_w4b():
+            src = w4_words[:, :, 2 * HALF : 4 * HALF].rearrange("g p c -> p g c")
+            nc.sync.dma_start(out=w4b[:].bitcast(I32), in_=src.bitcast(I32))
+
+        def load_w4_scales(eng, tile, h):
+            for q in range(4):
+                src = w4_scales[:, 4 * q : 4 * q + 4, HALF * h : HALF * (h + 1)].rearrange("g q n -> q g n")
+                eng.dma_start(out=tile[32 * q : 32 * q + 4, :, :].bitcast(I32), in_=src.bitcast(I32))
+
+        load_w4_scales(nc.scalar, w4sa, 0)
+        nc.scalar.copy(out=warm2[:], in_=warm[:])
+
+        load_x(2, 0)
+        load_w4a(0)
+        load_x(3, 0)
+        load_w4a(1)
+        load_x(4, 0)
+        load_w4a(2)
+        load_w4_scales(nc.sync, w4sb, 1)
+        load_w4b()
+        for q in range(4):
+            nc.sync.dma_start(
+                out=w8s[32 * q + 4 : 32 * q + 12, :].bitcast(I32),
+                in_=w8_scales[:, 4 * q : 4 * q + 4, :].bitcast(I32),
+            )
+        load_x(0, 0)
+        load_w8(0, 1)
+        load_x(1, 0)
+        load_w8(1, 1)
+        load_w8(0, 0)
+        load_w8(1, 0)
+        for g in (2, 3, 4, 0, 1):
+            load_x(g, 1)
+
+        QC = NT // 2
+
+        def prepare(g, h):
+            src = raw[g, h][:].rearrange("p j t -> p t j")
+            ga = stage.tile([P, QC, 4], BF16, name="ga", align_bytes=256)
+            gb = stage.tile([P, QC, 4], BF16, name="gb", align_bytes=256)
+            nc.vector.tensor_copy(out=ga[:], in_=src[:, 0:QC, :])
+            nc.scalar.copy(out=gb[:], in_=src[:, QC:NT, :])
+            for s, grp in ((slice(0, QC), ga), (slice(QC, NT), gb)):
+                nc.vector.quantize_mx(
+                    out=codes[g, h][:, s].bitcast(E4M3),
+                    scales=scales[g, h][:, s],
+                    in_=grp[:].rearrange("p t j -> p (t j)"),
+                )
+
+        def mm(acc, g, nh, j, th, start, stop):
+            cols = slice(P * j, P * (j + 1))
+            if g < 2:
+                lhs = w8[g, nh][:, cols].bitcast(E4M3)
+                k = 4 * (g + 1)
+                lhs_s = w8s[k:P, HALF * nh + P * j : HALF * nh + P * (j + 1)]
+            else:
+                bcols = slice(2 * P * j, 2 * P * (j + 1))
+                if nh == 0:
+                    lhs = w4a[g - 2][:, bcols].bitcast(E2M1)
+                    lhs_s = w4sa[:, g - 2, cols]
+                else:
+                    lhs = w4b[:, g - 2, bcols].bitcast(E2M1)
+                    lhs_s = w4sb[:, g - 2, cols]
+            nc.tensor.matmul_mx(
+                out=acc[:],
+                lhsT=lhs,
+                lhsT_scale=lhs_s,
+                rhs=codes[g, th][:].bitcast(E4M3),
+                rhs_scale=scales[g, th][:],
+                start=start,
+                stop=stop,
+            )
+
+        def bank():
+            acc = psum.tile([P, NT], F32, name="acc")
+            return acc
+
+        def copy_out(eng, acc, nh, j, th, part=None):
+            o = res.tile([P, NT], F32, name="o")
+            if eng == "v":
+                nc.vector.tensor_copy(out=o[:], in_=acc[:])
+            else:
+                nc.scalar.copy(out=o[:], in_=acc[:])
+            store(o, nh, j, th)
+
+        def store(o, nh, j, th):
+            r = HALF * nh + P * j
+            nc.sync.dma_start(out=out[r : r + P, NT * th : NT * (th + 1)], in_=o[:])
+
+        prepare(2, 0)
+        accs = [bank() for _ in range(TILES)]
+        for j in range(TILES):
+            mm(accs[j], 2, 0, j, 0, True, False)
+        prepare(3, 0)
+        for j in range(TILES):
+            mm(accs[j], 3, 0, j, 0, False, False)
+        prepare(4, 0)
+        for j in range(TILES):
+            mm(accs[j], 4, 0, j, 0, False, True)
+        spill = []
+        for j in range(TILES):
+            sp = keep.tile([P, NT], F32, name="spill_%d" % j)
+            if j % 3 == 1:
+                nc.vector.tensor_copy(out=sp[:], in_=accs[j][:])
+            else:
+                nc.scalar.copy(out=sp[:], in_=accs[j][:])
+            spill.append(sp)
+        accs = [bank() for _ in range(TILES)]
+        for j in range(TILES):
+            for g in (2, 3, 4):
+                mm(accs[j], g, 1, j, 0, g == 2, False)
+        prepare(0, 0)
+        for j in range(TILES):
+            mm(accs[j], 0, 1, j, 0, False, False)
+        prepare(1, 0)
+        for j in range(TILES):
+            mm(accs[j], 1, 1, j, 0, False, True)
+        for j in range(TILES):
+            copy_out("s" if j % 2 == 0 else "v", accs[j], 1, j, 0)
+        accs = [bank() for _ in range(TILES)]
+        for j in range(TILES):
+            for g in (0, 1):
+                mm(accs[j], g, 0, j, 0, g == 0, g == 1)
+            if j == 2:
+                prepare(2, 1)
+            if j == 5:
+                prepare(3, 1)
+            o = res.tile([P, NT], F32, name="o")
+            nc.vector.tensor_add(out=o[:], in0=accs[j][:], in1=spill[j][:])
+            store(o, 0, j, 0)
+        accs = [bank() for _ in range(TILES)]
+        for i, g in enumerate((2, 3, 4, 0, 1)):
+            if i >= 2:
+                prepare(g, 1)
+            for j in range(TILES):
+                mm(accs[j], g, 0, j, 1, i == 0, i == 4)
+        for j in range(TILES):
+            copy_out("s" if j % 2 == 0 else "v", accs[j], 0, j, 1)
+        for j in range(TILES):
+            acc = bank()
+            for i, g in enumerate((2, 3, 4, 0, 1)):
+                mm(acc, g, 1, j, 1, i == 0, i == 4)
+            if j < TILES - 1:
+                copy_out("s" if j % 2 == 0 else "v", acc, 1, j, 1)
+            else:
+                r = HALF + P * j
+                oa = res.tile([P, QC], F32, name="oa", bufs=1)
+                ob = res.tile([P, QC], F32, name="ob", bufs=1)
+                nc.vector.tensor_copy(out=oa[:], in_=acc[:, 0:QC])
+                nc.scalar.copy(out=ob[:], in_=acc[:, QC:NT])
+                nc.sync.dma_start(out=out[r : r + P, NT : NT + QC], in_=oa[:])
+                nc.scalar.dma_start(out=out[r : r + P, NT + QC : T], in_=ob[:])

@@ -25,7 +25,7 @@ def tile_mix_outl_fm_none_kernel(tc, x, w8_words, w8_scales, w4_words, w4_scales
     with ExitStack() as ctx:
         keep = ctx.enter_context(tc.tile_pool(name="keep", bufs=1))
         stage = ctx.enter_context(tc.tile_pool(name="stage", bufs=3))
-        res = ctx.enter_context(tc.tile_pool(name="res", bufs=12))
+        res = ctx.enter_context(tc.tile_pool(name="res", bufs=16))
         psum = ctx.enter_context(tc.psum_pool(name="psum", bufs=8))
         ctx.enter_context(tc.manual_schedule())
 
@@ -56,60 +56,75 @@ def tile_mix_outl_fm_none_kernel(tc, x, w8_words, w8_scales, w4_words, w4_scales
             rows = x[PASS * g : PASS * (g + 1), :].rearrange("(p j) t -> p j t", j=4)
             nc.sync.dma_start(out=raw[g, h][:], in_=rows[:, :, NT * h : NT * (h + 1)])
 
-        def load_w8(g, h):
-            src = w8_words[g].rearrange("p n i -> p (n i)")[:, 4 * HALF * h : 4 * HALF * (h + 1)]
-            nc.sync.dma_start(out=w8[g, h][:].bitcast(I32), in_=src.bitcast(I32))
+        def load_w8(g, h, lo=0, hi=TILES):
+            src = w8_words[g].rearrange("p n i -> p (n i)")[:, 4 * (HALF * h + P * lo) : 4 * (HALF * h + P * hi)]
+            nc.sync.dma_start(out=w8[g, h][:, P * lo : P * hi].bitcast(I32), in_=src.bitcast(I32))
 
         def load_w4a(g):
             nc.sync.dma_start(out=w4a[g][:].bitcast(I32), in_=w4_words[g][:, 0 : 2 * HALF].bitcast(I32))
-
-        def load_w4b():
-            src = w4_words[:, :, 2 * HALF : 4 * HALF].rearrange("g p c -> p g c")
-            nc.sync.dma_start(out=w4b[:].bitcast(I32), in_=src.bitcast(I32))
 
         def load_w4_scales(eng, tile, h):
             for q in range(4):
                 src = w4_scales[:, 4 * q : 4 * q + 4, HALF * h : HALF * (h + 1)].rearrange("g q n -> q g n")
                 eng.dma_start(out=tile[32 * q : 32 * q + 4, :, :].bitcast(I32), in_=src.bitcast(I32))
 
-        load_w4_scales(nc.scalar, w4sa, 0)
         nc.scalar.copy(out=warm2[:], in_=warm[:])
 
-        load_x(2, 0)
-        load_w4a(0)
-        load_x(3, 0)
-        load_w4a(1)
-        load_x(4, 0)
-        load_w4a(2)
-        load_w4_scales(nc.sync, w4sb, 1)
-        load_w4b()
-        for q in range(4):
-            nc.sync.dma_start(
-                out=w8s[32 * q + 4 : 32 * q + 12, :].bitcast(I32),
-                in_=w8_scales[:, 4 * q : 4 * q + 4, :].bitcast(I32),
-            )
+        def load_w4b(g):
+            nc.sync.dma_start(out=w4b[:, g, :].bitcast(I32), in_=w4_words[g][:, 2 * HALF : 4 * HALF].bitcast(I32))
+
+        def load_w8s():
+            for q in range(4):
+                nc.sync.dma_start(
+                    out=w8s[32 * q + 4 : 32 * q + 12, :].bitcast(I32),
+                    in_=w8_scales[:, 4 * q : 4 * q + 4, :].bitcast(I32),
+                )
+
         load_x(0, 0)
-        load_w8(0, 1)
+        load_w8s()
+        load_w8(0, 0, 0, 4)
         load_x(1, 0)
-        load_w8(1, 1)
-        load_w8(0, 0)
+        load_w8(0, 0, 4, 8)
         load_w8(1, 0)
-        for g in (2, 3, 4, 0, 1):
+        load_w8(0, 1)
+        load_w8(1, 1)
+        load_x(2, 0)
+        load_w4_scales(nc.sync, w4sb, 1)
+        load_w4b(0)
+        load_x(3, 0)
+        load_w4b(1)
+        load_x(4, 0)
+        load_w4b(2)
+        load_w4_scales(nc.sync, w4sa, 0)
+        for g in range(3):
+            load_w4a(g)
+        for g in range(5):
             load_x(g, 1)
 
         QC = NT // 2
 
-        def prepare(g, h):
+        grouped = {}
+
+        def group_v(g, h):
+            grp = stage.tile([P, NT, 4], BF16, name="grp", align_bytes=256)
+            grouped[g, h] = grp
             src = raw[g, h][:].rearrange("p j t -> p t j")
-            ga = stage.tile([P, QC, 4], BF16, name="ga", align_bytes=256)
-            gb = stage.tile([P, QC, 4], BF16, name="gb", align_bytes=256)
-            nc.vector.tensor_copy(out=ga[:], in_=src[:, 0:QC, :])
-            nc.scalar.copy(out=gb[:], in_=src[:, QC:NT, :])
-            for s, grp in ((slice(0, QC), ga), (slice(QC, NT), gb)):
+            nc.vector.tensor_copy(out=grp[:, 0:QC, :], in_=src[:, 0:QC, :])
+
+        def group_s(g, h):
+            nc.scalar.copy(out=grouped[g, h][:, QC:NT, :], in_=raw[g, h][:].rearrange("p j t -> p t j")[:, QC:NT, :])
+
+        def prepare(g, h):
+            group_v(g, h)
+            group_s(g, h)
+            quantize(g, h)
+
+        def quantize(g, h):
+            for s in (slice(0, QC), slice(QC, NT)):
                 nc.vector.quantize_mx(
                     out=codes[g, h][:, s].bitcast(E4M3),
                     scales=scales[g, h][:, s],
-                    in_=grp[:].rearrange("p t j -> p (t j)"),
+                    in_=grouped[g, h][:, s, :].rearrange("p t j -> p (t j)"),
                 )
 
         def mm(acc, g, nh, j, th, start, stop):
@@ -152,61 +167,61 @@ def tile_mix_outl_fm_none_kernel(tc, x, w8_words, w8_scales, w4_words, w4_scales
             r = HALF * nh + P * j
             nc.sync.dma_start(out=out[r : r + P, NT * th : NT * (th + 1)], in_=o[:])
 
-        prepare(2, 0)
+        prepare(0, 0)
         accs = [bank() for _ in range(TILES)]
         for j in range(TILES):
-            mm(accs[j], 2, 0, j, 0, True, False)
-        prepare(3, 0)
+            mm(accs[j], 0, 0, j, 0, True, False)
+        prepare(1, 0)
         for j in range(TILES):
-            mm(accs[j], 3, 0, j, 0, False, False)
-        prepare(4, 0)
-        for j in range(TILES):
-            mm(accs[j], 4, 0, j, 0, False, True)
+            mm(accs[j], 1, 0, j, 0, False, True)
         spill = []
         for j in range(TILES):
             sp = keep.tile([P, NT], F32, name="spill_%d" % j)
-            if j % 3 == 1:
+            if j % 2 == 0:
                 nc.vector.tensor_copy(out=sp[:], in_=accs[j][:])
             else:
                 nc.scalar.copy(out=sp[:], in_=accs[j][:])
             spill.append(sp)
         accs = [bank() for _ in range(TILES)]
         for j in range(TILES):
-            for g in (2, 3, 4):
-                mm(accs[j], g, 1, j, 0, g == 2, False)
-        prepare(0, 0)
-        for j in range(TILES):
-            mm(accs[j], 0, 1, j, 0, False, False)
-        prepare(1, 0)
-        for j in range(TILES):
-            mm(accs[j], 1, 1, j, 0, False, True)
-        for j in range(TILES):
-            copy_out("s" if j % 2 == 0 else "v", accs[j], 1, j, 0)
-        accs = [bank() for _ in range(TILES)]
-        for j in range(TILES):
             for g in (0, 1):
-                mm(accs[j], g, 0, j, 0, g == 0, g == 1)
-            if j == 2:
-                prepare(2, 1)
-            if j == 5:
-                prepare(3, 1)
-            o = res.tile([P, NT], F32, name="o")
-            nc.vector.tensor_add(out=o[:], in0=accs[j][:], in1=spill[j][:])
-            store(o, 0, j, 0)
+                mm(accs[j], g, 1, j, 0, g == 0, False)
+        for g in (2, 3, 4):
+            prepare(g, 0)
+            for j in range(TILES):
+                mm(accs[j], g, 1, j, 0, False, g == 4)
+        for j in range(TILES):
+            copy_out("v" if j % 2 == 0 else "s", accs[j], 1, j, 0)
         accs = [bank() for _ in range(TILES)]
-        for i, g in enumerate((2, 3, 4, 0, 1)):
-            if i >= 2:
+        for j in range(TILES):
+            for g in (2, 3, 4):
+                mm(accs[j], g, 0, j, 0, g == 2, g == 4)
+            nc.vector.tensor_add(out=spill[j][:], in0=accs[j][:], in1=spill[j][:])
+            store(spill[j], 0, j, 0)
+            if j == 0:
+                group_v(0, 1)
+                group_s(0, 1)
+            if j == 2:
+                quantize(0, 1)
+            if j == 5:
+                group_v(1, 1)
+                group_s(1, 1)
+        accs = [bank() for _ in range(TILES)]
+        for g in range(5):
+            if g == 1:
+                quantize(g, 1)
+            if g > 1:
                 prepare(g, 1)
             for j in range(TILES):
-                mm(accs[j], g, 0, j, 1, i == 0, i == 4)
+                mm(accs[j], g, 0, j, 1, g == 0, g == 4)
         for j in range(TILES):
-            copy_out("s" if j % 2 == 0 else "v", accs[j], 0, j, 1)
+            copy_out("v" if j % 2 == 0 else "s", accs[j], 0, j, 1)
         for j in range(TILES):
             acc = bank()
-            for i, g in enumerate((2, 3, 4, 0, 1)):
-                mm(acc, g, 1, j, 1, i == 0, i == 4)
+            for g in range(5):
+                mm(acc, g, 1, j, 1, g == 0, g == 4)
             if j < TILES - 1:
-                copy_out("s" if j % 2 == 0 else "v", acc, 1, j, 1)
+                copy_out("v" if j % 2 == 0 else "s", acc, 1, j, 1)
             else:
                 r = HALF + P * j
                 oa = res.tile([P, QC], F32, name="oa", bufs=1)

@@ -18,6 +18,7 @@ PASS = 512
 NT = 512
 HALF = M // 2
 TILES = HALF // P
+SPLIT_STORES = 1
 
 
 def tile_mix_outl_fm_none_kernel(tc, x, w8_words, w8_scales, w4_words, w4_scales, out):
@@ -39,7 +40,7 @@ def tile_mix_outl_fm_none_kernel(tc, x, w8_words, w8_scales, w4_words, w4_scales
         for g in range(2):
             for h in range(2):
                 w8[g, h] = keep.tile([P, HALF], U32, name="w8_%d_%d" % (g, h), align_bytes=256)
-        w4a = [keep.tile([P, 2 * HALF], U8, name="w4a_%d" % g, align_bytes=256) for g in range(3)]
+        w4a = keep.tile([P, 3, 2 * HALF], U8, name="w4a", align_bytes=256)
         w4b = keep.tile([P, 3, 2 * HALF], U8, name="w4b", align_bytes=256)
         w4sa = keep.tile([P, 3, HALF], U8, name="w4sa", align_bytes=256)
         w4sb = keep.tile([P, 3, HALF], U8, name="w4sb", align_bytes=256)
@@ -60,8 +61,9 @@ def tile_mix_outl_fm_none_kernel(tc, x, w8_words, w8_scales, w4_words, w4_scales
             src = w8_words[g].rearrange("p n i -> p (n i)")[:, 4 * (HALF * h + P * lo) : 4 * (HALF * h + P * hi)]
             nc.sync.dma_start(out=w8[g, h][:, P * lo : P * hi].bitcast(I32), in_=src.bitcast(I32))
 
-        def load_w4a(g):
-            nc.sync.dma_start(out=w4a[g][:].bitcast(I32), in_=w4_words[g][:, 0 : 2 * HALF].bitcast(I32))
+        def load_w4a():
+            src = w4_words[:, :, 0 : 2 * HALF].rearrange("g p c -> p g c")
+            nc.sync.dma_start(out=w4a[:].bitcast(I32), in_=src.bitcast(I32))
 
         def load_w4_scales(eng, tile, h):
             for q in range(4):
@@ -95,9 +97,8 @@ def tile_mix_outl_fm_none_kernel(tc, x, w8_words, w8_scales, w4_words, w4_scales
         load_w4b(1)
         load_x(4, 0)
         load_w4b(2)
+        load_w4a()
         load_w4_scales(nc.sync, w4sa, 0)
-        for g in range(3):
-            load_w4a(g)
         for g in range(5):
             load_x(g, 1)
 
@@ -136,7 +137,7 @@ def tile_mix_outl_fm_none_kernel(tc, x, w8_words, w8_scales, w4_words, w4_scales
             else:
                 bcols = slice(2 * P * j, 2 * P * (j + 1))
                 if nh == 0:
-                    lhs = w4a[g - 2][:, bcols].bitcast(E2M1)
+                    lhs = w4a[:, g - 2, bcols].bitcast(E2M1)
                     lhs_s = w4sa[:, g - 2, cols]
                 else:
                     lhs = w4b[:, g - 2, bcols].bitcast(E2M1)
@@ -176,11 +177,11 @@ def tile_mix_outl_fm_none_kernel(tc, x, w8_words, w8_scales, w4_words, w4_scales
             mm(accs[j], 1, 0, j, 0, False, True)
         spill = []
         for j in range(TILES):
-            sp = keep.tile([P, NT], F32, name="spill_%d" % j)
+            sp = keep.tile([P, T], F32, name="spill_%d" % j, align_bytes=256)
             if j % 2 == 0:
-                nc.vector.tensor_copy(out=sp[:], in_=accs[j][:])
+                nc.vector.tensor_copy(out=sp[:, 0:NT], in_=accs[j][:])
             else:
-                nc.scalar.copy(out=sp[:], in_=accs[j][:])
+                nc.scalar.copy(out=sp[:, 0:NT], in_=accs[j][:])
             spill.append(sp)
         accs = [bank() for _ in range(TILES)]
         for j in range(TILES):
@@ -196,8 +197,9 @@ def tile_mix_outl_fm_none_kernel(tc, x, w8_words, w8_scales, w4_words, w4_scales
         for j in range(TILES):
             for g in (2, 3, 4):
                 mm(accs[j], g, 0, j, 0, g == 2, g == 4)
-            nc.vector.tensor_add(out=spill[j][:], in0=accs[j][:], in1=spill[j][:])
-            store(spill[j], 0, j, 0)
+            nc.vector.tensor_add(out=spill[j][:, 0:NT], in0=accs[j][:], in1=spill[j][:, 0:NT])
+            if j < SPLIT_STORES:
+                nc.sync.dma_start(out=out[P * j : P * (j + 1), 0:NT], in_=spill[j][:, 0:NT])
             if j == 0:
                 group_v(0, 1)
                 group_s(0, 1)
@@ -215,7 +217,12 @@ def tile_mix_outl_fm_none_kernel(tc, x, w8_words, w8_scales, w4_words, w4_scales
             for j in range(TILES):
                 mm(accs[j], g, 0, j, 1, g == 0, g == 4)
         for j in range(TILES):
-            copy_out("v" if j % 2 == 0 else "s", accs[j], 0, j, 1)
+            if j % 2 == 0:
+                nc.vector.tensor_copy(out=spill[j][:, NT:T], in_=accs[j][:])
+            else:
+                nc.scalar.copy(out=spill[j][:, NT:T], in_=accs[j][:])
+            lo = NT if j < SPLIT_STORES else 0
+            nc.sync.dma_start(out=out[P * j : P * (j + 1), lo:T], in_=spill[j][:, lo:T])
         for j in range(TILES):
             acc = bank()
             for g in range(5):

@@ -19,6 +19,8 @@ NT = 512
 HALF = M // 2
 TILES = HALF // P
 SPLIT_STORES = 1
+HOLD = 8
+QS = 1
 
 
 def tile_mix_outl_fm_none_kernel(tc, x, w8_words, w8_scales, w4_words, w4_scales, out):
@@ -30,7 +32,7 @@ def tile_mix_outl_fm_none_kernel(tc, x, w8_words, w8_scales, w4_words, w4_scales
         psum = ctx.enter_context(tc.psum_pool(name="psum", bufs=8))
         ctx.enter_context(tc.manual_schedule())
 
-        raw, codes, scales = {}, {}, {}
+        raw, codes, scales, held = {}, {}, {}, {}
         for g in range(5):
             for h in range(2):
                 raw[g, h] = keep.tile([P, 4, NT], F32, name="raw_%d_%d" % (g, h), align_bytes=256)
@@ -38,42 +40,37 @@ def tile_mix_outl_fm_none_kernel(tc, x, w8_words, w8_scales, w4_words, w4_scales
                 scales[g, h] = keep.tile([P, NT], U8, name="scales_%d_%d" % (g, h), align_bytes=256)
         w8 = {}
         for g in range(2):
-            for h in range(2):
-                w8[g, h] = keep.tile([P, HALF], U32, name="w8_%d_%d" % (g, h), align_bytes=256)
-        w4a = keep.tile([P, 3, 2 * HALF], U8, name="w4a", align_bytes=256)
-        w4b = keep.tile([P, 3, 2 * HALF], U8, name="w4b", align_bytes=256)
-        w4sa = keep.tile([P, 3, HALF], U8, name="w4sa", align_bytes=256)
-        w4sb = keep.tile([P, 3, HALF], U8, name="w4sb", align_bytes=256)
+            w8[g] = keep.tile([P, M], U32, name="w8_%d" % g, align_bytes=256)
+        w4 = [keep.tile([P, 2 * M], U8, name="w4_%d" % g, align_bytes=256) for g in range(3)]
+        w4s = [keep.tile([P, 3, HALF], U8, name="w4s_%d" % h, align_bytes=256) for h in range(2)]
         w8s = keep.tile([P, M], U8, name="w8s", align_bytes=256)
         warm = keep.tile([P, 8], F32, name="warm")
         warm2 = keep.tile([P, 8], F32, name="warm2")
 
-        nc.vector.memset(w4sa[:].rearrange("p g n -> p (g n)").bitcast(U32), 0)
         nc.gpsimd.memset(warm[:], 0.0)
         nc.gpsimd.memset(w8s[:].bitcast(U32), 0)
-        nc.gpsimd.memset(w4sb[:].rearrange("p g n -> p (g n)").bitcast(U32), 0)
+        for h in (1, 0):
+            nc.gpsimd.memset(w4s[h][:].rearrange("p g n -> p (g n)").bitcast(U32), 0)
 
         def load_x(g, h):
             rows = x[PASS * g : PASS * (g + 1), :].rearrange("(p j) t -> p j t", j=4)
             nc.sync.dma_start(out=raw[g, h][:], in_=rows[:, :, NT * h : NT * (h + 1)])
 
-        def load_w8(g, h, lo=0, hi=TILES):
-            src = w8_words[g].rearrange("p n i -> p (n i)")[:, 4 * (HALF * h + P * lo) : 4 * (HALF * h + P * hi)]
-            nc.sync.dma_start(out=w8[g, h][:, P * lo : P * hi].bitcast(I32), in_=src.bitcast(I32))
+        def load_w8(g, lo, hi):
+            src = w8_words[g].rearrange("p n i -> p (n i)")[:, 4 * lo : 4 * hi]
+            nc.sync.dma_start(out=w8[g][:, lo:hi].bitcast(I32), in_=src.bitcast(I32))
 
-        def load_w4a():
-            src = w4_words[:, :, 0 : 2 * HALF].rearrange("g p c -> p g c")
-            nc.sync.dma_start(out=w4a[:].bitcast(I32), in_=src.bitcast(I32))
+        def load_w4(g0, g1, lo, hi):
+            for g in range(g0, g1):
+                src = w4_words[g][:, 2 * lo : 2 * hi]
+                nc.sync.dma_start(out=w4[g][:, 2 * lo : 2 * hi].bitcast(I32), in_=src.bitcast(I32))
 
-        def load_w4_scales(eng, tile, h):
+        def load_w4_scales(lo, hi):
             for q in range(4):
-                src = w4_scales[:, 4 * q : 4 * q + 4, HALF * h : HALF * (h + 1)].rearrange("g q n -> q g n")
-                eng.dma_start(out=tile[32 * q : 32 * q + 4, :, :].bitcast(I32), in_=src.bitcast(I32))
+                src = w4_scales[:, 4 * q : 4 * q + 4, lo:hi].rearrange("g q n -> q g n")
+                nc.sync.dma_start(out=w4s[lo // HALF][32 * q : 32 * q + 4, :, :].bitcast(I32), in_=src.bitcast(I32))
 
         nc.scalar.copy(out=warm2[:], in_=warm[:])
-
-        def load_w4b(g):
-            nc.sync.dma_start(out=w4b[:, g, :].bitcast(I32), in_=w4_words[g][:, 2 * HALF : 4 * HALF].bitcast(I32))
 
         def load_w8s():
             for q in range(4):
@@ -84,24 +81,21 @@ def tile_mix_outl_fm_none_kernel(tc, x, w8_words, w8_scales, w4_words, w4_scales
 
         load_x(0, 0)
         load_w8s()
-        load_w8(0, 0, 0, 4)
+        load_w8(0, 0, HALF)
         load_x(1, 0)
-        load_w8(0, 0, 4, 8)
-        load_w8(1, 0)
-        load_w8(0, 1)
-        load_w8(1, 1)
+        load_w8(1, 0, M)
+        load_w8(0, HALF, M)
         load_x(2, 0)
-        load_w4_scales(nc.sync, w4sb, 1)
-        load_w4b(0)
+        load_w4_scales(HALF, M)
+        load_w4(0, 1, HALF, M)
         load_x(3, 0)
-        load_w4b(1)
+        load_w4(1, 2, HALF, M)
         load_x(4, 0)
-        load_w4b(2)
-        load_w4a()
-        load_w4_scales(nc.sync, w4sa, 0)
+        load_w4(2, 3, 0, M)
+        load_w4(0, 2, 0, HALF)
+        load_w4_scales(0, HALF)
         for g in range(5):
             load_x(g, 1)
-
         QC = NT // 2
 
         grouped = {}
@@ -129,19 +123,14 @@ def tile_mix_outl_fm_none_kernel(tc, x, w8_words, w8_scales, w4_words, w4_scales
                 )
 
         def mm(acc, g, nh, j, th, start, stop):
-            cols = slice(P * j, P * (j + 1))
             if g < 2:
-                lhs = w8[g, nh][:, cols].bitcast(E4M3)
+                lhs = w8[g][:, HALF * nh + P * j : HALF * nh + P * (j + 1)].bitcast(E4M3)
                 k = 4 * (g + 1)
                 lhs_s = w8s[k:P, HALF * nh + P * j : HALF * nh + P * (j + 1)]
             else:
-                bcols = slice(2 * P * j, 2 * P * (j + 1))
-                if nh == 0:
-                    lhs = w4a[:, g - 2, bcols].bitcast(E2M1)
-                    lhs_s = w4sa[:, g - 2, cols]
-                else:
-                    lhs = w4b[:, g - 2, bcols].bitcast(E2M1)
-                    lhs_s = w4sb[:, g - 2, cols]
+                n0 = HALF * nh + P * j
+                lhs = w4[g - 2][:, 2 * n0 : 2 * (n0 + P)].bitcast(E2M1)
+                lhs_s = w4s[nh][:, g - 2, P * j : P * (j + 1)]
             nc.tensor.matmul_mx(
                 out=acc[:],
                 lhsT=lhs,
@@ -162,11 +151,11 @@ def tile_mix_outl_fm_none_kernel(tc, x, w8_words, w8_scales, w4_words, w4_scales
                 nc.vector.tensor_copy(out=o[:], in_=acc[:])
             else:
                 nc.scalar.copy(out=o[:], in_=acc[:])
-            store(o, nh, j, th)
+            store(o, nh, j, th, nc.scalar if QS and eng == "s" and th == 1 else nc.sync)
 
-        def store(o, nh, j, th):
+        def store(o, nh, j, th, queue=None):
             r = HALF * nh + P * j
-            nc.sync.dma_start(out=out[r : r + P, NT * th : NT * (th + 1)], in_=o[:])
+            (queue or nc.sync).dma_start(out=out[r : r + P, NT * th : NT * (th + 1)], in_=o[:])
 
         prepare(0, 0)
         accs = [bank() for _ in range(TILES)]
@@ -192,7 +181,15 @@ def tile_mix_outl_fm_none_kernel(tc, x, w8_words, w8_scales, w4_words, w4_scales
             for j in range(TILES):
                 mm(accs[j], g, 1, j, 0, False, g == 4)
         for j in range(TILES):
-            copy_out("v" if j % 2 == 0 else "s", accs[j], 1, j, 0)
+            if j >= HOLD:
+                hold = keep.tile([P, T], F32, name="hold_%d" % j, align_bytes=256)
+                held[j] = hold
+                if j % 2 == 0:
+                    nc.vector.tensor_copy(out=hold[:, 0:NT], in_=accs[j][:])
+                else:
+                    nc.scalar.copy(out=hold[:, 0:NT], in_=accs[j][:])
+            else:
+                copy_out("v" if j % 2 == 0 else "s", accs[j], 1, j, 0)
         accs = [bank() for _ in range(TILES)]
         for j in range(TILES):
             for g in (2, 3, 4):
@@ -222,12 +219,19 @@ def tile_mix_outl_fm_none_kernel(tc, x, w8_words, w8_scales, w4_words, w4_scales
             else:
                 nc.scalar.copy(out=spill[j][:, NT:T], in_=accs[j][:])
             lo = NT if j < SPLIT_STORES else 0
-            nc.sync.dma_start(out=out[P * j : P * (j + 1), lo:T], in_=spill[j][:, lo:T])
+            (nc.scalar if QS and j % 2 == 1 else nc.sync).dma_start(out=out[P * j : P * (j + 1), lo:T], in_=spill[j][:, lo:T])
         for j in range(TILES):
             acc = bank()
             for g in range(5):
                 mm(acc, g, 1, j, 1, g == 0, g == 4)
-            if j < TILES - 1:
+            if j in held:
+                hold = held[j]
+                if j % 2 == 0:
+                    nc.vector.tensor_copy(out=hold[:, NT:T], in_=acc[:])
+                else:
+                    nc.scalar.copy(out=hold[:, NT:T], in_=acc[:])
+                nc.sync.dma_start(out=out[HALF + P * j : HALF + P * (j + 1), :], in_=hold[:])
+            elif j < TILES - 1:
                 copy_out("v" if j % 2 == 0 else "s", acc, 1, j, 1)
             else:
                 r = HALF + P * j

from contextlib import ExitStack

import concourse.mybir as mybir

O, K, M, T = 1024, 2560, 2048, 1024
FLOPS = 2 * K * M * T

F32 = mybir.dt.float32
BF16 = mybir.dt.bfloat16
I32 = mybir.dt.int32
U32 = mybir.dt.uint32
U8 = mybir.dt.uint8
E4M3 = mybir.dt.float8_e4m3fn_x4
E2M1 = mybir.dt.float4_e2m1fn_x4

P = 128
PASS = 512
NT = 512
HALF = M // 2
TILES = HALF // P
SPLIT_STORES = 1
HOLD = 8
QS = 1


def tile_mix_outl_fm_none_kernel(tc, x, w8_words, w8_scales, w4_words, w4_scales, out):
    nc = tc.nc
    with ExitStack() as ctx:
        keep = ctx.enter_context(tc.tile_pool(name="keep", bufs=1))
        stage = ctx.enter_context(tc.tile_pool(name="stage", bufs=3))
        res = ctx.enter_context(tc.tile_pool(name="res", bufs=16))
        psum = ctx.enter_context(tc.psum_pool(name="psum", bufs=8))
        ctx.enter_context(tc.manual_schedule())

        raw, codes, scales, held = {}, {}, {}, {}
        for g in range(5):
            for h in range(2):
                raw[g, h] = keep.tile([P, 4, NT], F32, name="raw_%d_%d" % (g, h), align_bytes=256)
                codes[g, h] = keep.tile([P, NT], U32, name="codes_%d_%d" % (g, h), align_bytes=256)
                scales[g, h] = keep.tile([P, NT], U8, name="scales_%d_%d" % (g, h), align_bytes=256)
        w8 = {}
        for g in range(2):
            w8[g] = keep.tile([P, M], U32, name="w8_%d" % g, align_bytes=256)
        w4 = [keep.tile([P, 2 * M], U8, name="w4_%d" % g, align_bytes=256) for g in range(3)]
        w4s = [keep.tile([P, 3, HALF], U8, name="w4s_%d" % h, align_bytes=256) for h in range(2)]
        w8s = keep.tile([P, M], U8, name="w8s", align_bytes=256)
        warm = keep.tile([P, 8], F32, name="warm")
        warm2 = keep.tile([P, 8], F32, name="warm2")

        nc.gpsimd.memset(warm[:], 0.0)
        nc.gpsimd.memset(w8s[:].bitcast(U32), 0)
        for h in (1, 0):
            nc.gpsimd.memset(w4s[h][:].rearrange("p g n -> p (g n)").bitcast(U32), 0)

        def load_x(g, h):
            rows = x[PASS * g : PASS * (g + 1), :].rearrange("(p j) t -> p j t", j=4)
            nc.sync.dma_start(out=raw[g, h][:], in_=rows[:, :, NT * h : NT * (h + 1)])

        def load_w8(g, lo, hi):
            src = w8_words[g].rearrange("p n i -> p (n i)")[:, 4 * lo : 4 * hi]
            nc.sync.dma_start(out=w8[g][:, lo:hi].bitcast(I32), in_=src.bitcast(I32))

        def load_w4(g0, g1, lo, hi):
            for g in range(g0, g1):
                src = w4_words[g][:, 2 * lo : 2 * hi]
                nc.sync.dma_start(out=w4[g][:, 2 * lo : 2 * hi].bitcast(I32), in_=src.bitcast(I32))

        def load_w4_scales(lo, hi):
            for q in range(4):
                src = w4_scales[:, 4 * q : 4 * q + 4, lo:hi].rearrange("g q n -> q g n")
                nc.sync.dma_start(out=w4s[lo // HALF][32 * q : 32 * q + 4, :, :].bitcast(I32), in_=src.bitcast(I32))

        nc.scalar.copy(out=warm2[:], in_=warm[:])

        def load_w8s():
            for q in range(4):
                nc.sync.dma_start(
                    out=w8s[32 * q + 4 : 32 * q + 12, :].bitcast(I32),
                    in_=w8_scales[:, 4 * q : 4 * q + 4, :].bitcast(I32),
                )

        load_x(0, 0)
        load_w8s()
        load_w8(0, 0, HALF)
        load_x(1, 0)
        load_w8(1, 0, M)
        load_w8(0, HALF, M)
        load_x(2, 0)
        load_w4_scales(HALF, M)
        load_w4(0, 1, HALF, M)
        load_x(3, 0)
        load_w4(1, 2, HALF, M)
        load_x(4, 0)
        load_w4(2, 3, 0, M)
        load_w4(0, 2, 0, HALF)
        load_w4_scales(0, HALF)
        for g in range(5):
            load_x(g, 1)
        QC = NT // 2

        grouped = {}

        def group_v(g, h):
            grp = stage.tile([P, NT, 4], BF16, name="grp", align_bytes=256)
            grouped[g, h] = grp
            src = raw[g, h][:].rearrange("p j t -> p t j")
            nc.vector.tensor_copy(out=grp[:, 0:QC, :], in_=src[:, 0:QC, :])

        def group_s(g, h):
            nc.scalar.copy(out=grouped[g, h][:, QC:NT, :], in_=raw[g, h][:].rearrange("p j t -> p t j")[:, QC:NT, :])

        def prepare(g, h):
            group_v(g, h)
            group_s(g, h)
            quantize(g, h)

        def quantize(g, h):
            for s in (slice(0, QC), slice(QC, NT)):
                nc.vector.quantize_mx(
                    out=codes[g, h][:, s].bitcast(E4M3),
                    scales=scales[g, h][:, s],
                    in_=grouped[g, h][:, s, :].rearrange("p t j -> p (t j)"),
                )

        def mm(acc, g, nh, j, th, start, stop):
            if g < 2:
                lhs = w8[g][:, HALF * nh + P * j : HALF * nh + P * (j + 1)].bitcast(E4M3)
                k = 4 * (g + 1)
                lhs_s = w8s[k:P, HALF * nh + P * j : HALF * nh + P * (j + 1)]
            else:
                n0 = HALF * nh + P * j
                lhs = w4[g - 2][:, 2 * n0 : 2 * (n0 + P)].bitcast(E2M1)
                lhs_s = w4s[nh][:, g - 2, P * j : P * (j + 1)]
            nc.tensor.matmul_mx(
                out=acc[:],
                lhsT=lhs,
                lhsT_scale=lhs_s,
                rhs=codes[g, th][:].bitcast(E4M3),
                rhs_scale=scales[g, th][:],
                start=start,
                stop=stop,
            )

        def bank():
            acc = psum.tile([P, NT], F32, name="acc")
            return acc

        def copy_out(eng, acc, nh, j, th, part=None):
            o = res.tile([P, NT], F32, name="o")
            if eng == "v":
                nc.vector.tensor_copy(out=o[:], in_=acc[:])
            else:
                nc.scalar.copy(out=o[:], in_=acc[:])
            store(o, nh, j, th, nc.scalar if QS and eng == "s" and th == 1 else nc.sync)

        def store(o, nh, j, th, queue=None):
            r = HALF * nh + P * j
            (queue or nc.sync).dma_start(out=out[r : r + P, NT * th : NT * (th + 1)], in_=o[:])

        prepare(0, 0)
        accs = [bank() for _ in range(TILES)]
        for j in range(TILES):
            mm(accs[j], 0, 0, j, 0, True, False)
        prepare(1, 0)
        for j in range(TILES):
            mm(accs[j], 1, 0, j, 0, False, True)
        spill = []
        for j in range(TILES):
            sp = keep.tile([P, T], F32, name="spill_%d" % j, align_bytes=256)
            if j % 2 == 0:
                nc.vector.tensor_copy(out=sp[:, 0:NT], in_=accs[j][:])
            else:
                nc.scalar.copy(out=sp[:, 0:NT], in_=accs[j][:])
            spill.append(sp)
        accs = [bank() for _ in range(TILES)]
        for j in range(TILES):
            for g in (0, 1):
                mm(accs[j], g, 1, j, 0, g == 0, False)
        for g in (2, 3, 4):
            prepare(g, 0)
            for j in range(TILES):
                mm(accs[j], g, 1, j, 0, False, g == 4)
        for j in range(TILES):
            if j >= HOLD:
                hold = keep.tile([P, T], F32, name="hold_%d" % j, align_bytes=256)
                held[j] = hold
                if j % 2 == 0:
                    nc.vector.tensor_copy(out=hold[:, 0:NT], in_=accs[j][:])
                else:
                    nc.scalar.copy(out=hold[:, 0:NT], in_=accs[j][:])
            else:
                copy_out("v" if j % 2 == 0 else "s", accs[j], 1, j, 0)
        accs = [bank() for _ in range(TILES)]
        for j in range(TILES):
            for g in (2, 3, 4):
                mm(accs[j], g, 0, j, 0, g == 2, g == 4)
            nc.vector.tensor_add(out=spill[j][:, 0:NT], in0=accs[j][:], in1=spill[j][:, 0:NT])
            if j < SPLIT_STORES:
                nc.sync.dma_start(out=out[P * j : P * (j + 1), 0:NT], in_=spill[j][:, 0:NT])
            if j == 0:
                group_v(0, 1)
                group_s(0, 1)
            if j == 2:
                quantize(0, 1)
            if j == 5:
                group_v(1, 1)
                group_s(1, 1)
        accs = [bank() for _ in range(TILES)]
        for g in range(5):
            if g == 1:
                quantize(g, 1)
            if g > 1:
                prepare(g, 1)
            for j in range(TILES):
                mm(accs[j], g, 0, j, 1, g == 0, g == 4)
        for j in range(TILES):
            if j % 2 == 0:
                nc.vector.tensor_copy(out=spill[j][:, NT:T], in_=accs[j][:])
            else:
                nc.scalar.copy(out=spill[j][:, NT:T], in_=accs[j][:])
            lo = NT if j < SPLIT_STORES else 0
            (nc.scalar if QS and j % 2 == 1 else nc.sync).dma_start(out=out[P * j : P * (j + 1), lo:T], in_=spill[j][:, lo:T])
        for j in range(TILES):
            acc = bank()
            for g in range(5):
                mm(acc, g, 1, j, 1, g == 0, g == 4)
            if j in held:
                hold = held[j]
                if j % 2 == 0:
                    nc.vector.tensor_copy(out=hold[:, NT:T], in_=acc[:])
                else:
                    nc.scalar.copy(out=hold[:, NT:T], in_=acc[:])
                nc.sync.dma_start(out=out[HALF + P * j : HALF + P * (j + 1), :], in_=hold[:])
            elif j < TILES - 1:
                copy_out("v" if j % 2 == 0 else "s", acc, 1, j, 1)
            else:
                r = HALF + P * j
                oa = res.tile([P, QC], F32, name="oa", bufs=1)
                ob = res.tile([P, QC], F32, name="ob", bufs=1)
                nc.vector.tensor_copy(out=oa[:], in_=acc[:, 0:QC])
                nc.scalar.copy(out=ob[:], in_=acc[:, QC:NT])
                nc.sync.dma_start(out=out[r : r + P, NT : NT + QC], in_=oa[:])
                nc.scalar.dma_start(out=out[r : r + P, NT + QC : T], in_=ob[:])
